import numpy as np, ml_dtypes
CORES = [25,29,65,69,153,157,193,197]
N = 8
import mx_ref
BF = ml_dtypes.bfloat16
def entries(a):
    return np.ascontiguousarray(a.T).reshape(-1)
def table(e):
    return np.ascontiguousarray(np.reshape(e, (-1, 16)).T).astype(np.int32)
def gentries(a):
    return np.ascontiguousarray(a.reshape(8, 16, -1).transpose(0, 2, 1)).reshape(8, -1)
def gtable(e):
    e = np.asarray(e); return np.ascontiguousarray(e.reshape(8, -1, 16).transpose(0, 2, 1)).reshape(128, -1).astype(np.int32)
def gcols(t, e):
    v = np.concatenate([t.reshape(8, 16, -1, 4), np.zeros((8, 16, 1, 4), BF)], axis=2)
    return np.ascontiguousarray(np.stack([v[g][:, e[g]] for g in range(8)])).reshape(128, -1)
def tile(rs):
    return np.stack(rs, axis=2).reshape(128, -1).astype(BF)
def pick(q, e):
    c = np.concatenate([q[0].reshape(128, -1, 4), np.zeros((128, 1, 4), np.uint8)], axis=1); s = np.concatenate([q[1], np.ones((16, 1), np.uint8)], axis=1)
    return (np.ascontiguousarray(c[:, e].reshape(128, -1)), np.ascontiguousarray(s[:, e]))
def join(*qs):
    return (np.concatenate([q[0] for q in qs], axis=1), np.concatenate([q[1] for q in qs], axis=1))
def put(q, e, v):
    c, s = q[0].reshape(128, -1, 4).copy(), q[1].copy(); c[:, e] = v[0].reshape(128, -1, 4); s[:, e] = v[1]
    return (c.reshape(128, -1), s)
def pk(c, s):
    return (np.ascontiguousarray(c), mx_ref.live(s))
def emit(q):
    return q[0], q[1]
def packed(v, rng):
    q = [mx_ref.quantize(np.ascontiguousarray(v[r])) for r in range(N)]
    return np.stack([a for a, b in q]), np.stack([mx_ref.plane(b, rng) for a, b in q])
def values_of_codes():
    e, c = np.zeros((128, 128, 4), np.float32), np.zeros((128, 2, 4), np.uint8)
    e[np.arange(128), np.arange(128), 0] = 1
    c[:127, :, 0] = np.arange(256).reshape(2, 128).T[:127]
    return mx_ref.matmul(mx_ref.quantize(e.reshape(128, 512).astype(BF)), (c.reshape(128, 8), np.full((16, 2), 127, np.uint8))).T.reshape(-1).astype(np.float64)
CODE_VALUE, SCALE_VALUE = values_of_codes(), 2.0 ** (np.arange(256) - 127.0)
def decode(q):
    return (CODE_VALUE[q[0]].reshape(16, 8, -1, 4) * SCALE_VALUE[q[1]][:, None, :, None] + 0.0).reshape(128, -1).astype(np.float32)
def f(rng, *shape):
    return mx_ref.flush((rng.standard_normal(shape, dtype=np.float32) * np.exp2(rng.integers(-2, 3, shape[:-1] + (1,)))).astype(BF))
def wide(rng, *shape, cols=0):
    v = rng.standard_normal(shape, dtype=np.float32) * np.exp2(rng.integers(-12, 13, shape)).astype(np.float32)
    if cols: v *= np.repeat(np.exp2(rng.integers(-cols, cols + 1, shape[:-2] + (1, shape[-1] // 4))) * (rng.random(shape[:-2] + (1, shape[-1] // 4)) > 0.0625), 4, axis=-1).astype(np.float32)
    return mx_ref.flush(v.astype(BF))
C = 320
STEP = [4, 1, 2]
def numbers_of(rng):
    return {"x": np.array(f(rng, N, 128, 4 * C)), "u": np.array(f(rng, N, 128, 512)), "v": np.array(f(rng, N, 128, 512))}
def orders(rng):
    return rng.permuted(np.tile(np.arange(C), (N, 1)), axis=1)
def pairing(rng):
    p = rng.permuted(np.tile(np.arange(C), (N, 8, 1)), axis=2)
    m = np.zeros((N, 8, C), np.int64)
    np.put_along_axis(m, p[:, :, ::2], p[:, :, 1::2], axis=2)
    np.put_along_axis(m, p[:, :, 1::2], p[:, :, ::2], axis=2)
    return m
def stored(a, t, m):
    return {"la": np.stack([table(a[r]) for r in range(N)]), "lb": np.stack([table(t[r]) for r in range(N)]), "mt": np.stack([gtable(m[r]) for r in range(N)])}
def lists(rng):
    return stored(orders(rng), orders(rng), pairing(rng))
def layers(rng, still=[]):
    w = np.array(f(rng, N, 128, 2048)).reshape(N, 8, 16, 4, 8, 16, 4)
    for i in still:
        w[:, :, i] = 0
        w[:, :, :, :, :, i] = 0
    return w
def weights(rng, w):
    c, p = packed(np.ascontiguousarray(w).reshape(N, 128, 2048), rng)
    return {"wc": c, "ws": p}
def setup_inputs(rng):
    return {**numbers_of(rng), **lists(rng), **weights(rng, layers(rng))}
def setup_inputs_ties(rng):
    d = numbers_of(rng)
    m = pairing(rng)
    o = rng.permutation(N)
    k = rng.integers(0, 4, (N, 8, C))
    k[o[1]] += 1
    k[o[2]] = (np.arange(C) > m[o[2]]) == (rng.permutation(8) < 4)[:, None]
    k[o[3]] = 1
    h = rng.permutation(8)
    k[o[3], h[:4], C - 1] = 2
    k[o[3], h[4:], 0] = 0
    x = d["x"].reshape(N, 8, 16, C, 4)
    x[:, :, 0] = 0
    x[:, :, 0, :, 0] = k.astype(np.float32).astype(BF)
    a = np.tile(np.exp2(rng.integers(-3, 4, (1, 8, 1)).astype(np.float32)), (N, 1, C))
    x[:, :, 8:] = 0
    x[:, :, 8, :, 0] = (-1.125 * a).astype(BF)
    x[:, :, 10, :, 0] = (-0.0703125 * a).astype(BF)
    u = d["u"].reshape(N, 128, 128, 4)
    u[:, :, ::16] = 0
    for r in range(N):
        for i in range(0, 128, 16): u[r, i, i, 0] = 0.0 if r == o[0] else -1.0 if r == o[1] else 1.0
    w = layers(rng, [0])
    w[:, :, :, :, :, 8:] = 0
    for g in range(8):
        w[:, g, 8, 0, g, 8, 0] = -28.0
        for b in range(4): w[:, g, 10, b, g, 9, 0] = -2.0 ** (b - 5)
    return {"x": x.reshape(N, 128, 4 * C), "u": u.reshape(N, 128, 512), "v": d["v"], **stored(orders(rng), orders(rng), m), **weights(rng, w)}
def setup_inputs_near(rng):
    d = numbers_of(rng)
    o = np.zeros(N, np.int64)
    for n, r in enumerate(rng.permutation([r for r in range(N) if r < r ^ STEP[0]])):
        e = rng.integers(2)
        o[r], o[r ^ STEP[0]] = n % 2 * 2 + e, n % 2 * 2 + 1 - e
    x = d["x"].astype(np.float32).reshape(N, 8, 16, C, 4)
    x[:, :, 0] = 0
    x[:, :, 8:] = 0
    u = d["u"].reshape(N, 128, 128, 4)
    u[:, :, ::16] = 0
    w = layers(rng, [0, 1, 8, 9, 10, 11, 12, 13, 14, 15])
    for r in range(N):
        c = rng.choice([-1.0, 1.0], (8, 1))
        s = rng.integers(0, 16, (8, C))
        digits = ((s[:, :, None] >> np.arange(4)) & 1) * np.exp2(np.arange(4) - 23.0)
        if o[r] < 2:
            x[r, :, 0, :, 0] = c
            x[r, :, 8] = digits
            x[r, :, 11, :, 0] = 2.0 ** -10
        elif o[r] == 2:
            x[r, :, 8] = digits * rng.choice([-1.0, 1.0], (8, C, 1))
            x[r, :, 1:8] = 0
            x[r, :, 1, :, 0] = rng.choice([-1.0, 1.0], (8, C)) * 2.0 ** -30
            for g in range(8):
                w[r, g, 1, 0, g, 12, 0] = 2.0 ** -8
                w[r, g, 1, 0, g, 13, 0] = 64.0
        else:
            x[r, :, 8, :, 0] = np.where(s < 8, 1.25, 0.0) * 2.0 ** -30 * c
            x[r, :, 9, :, 0] = np.where(s < 8, 0.0, 1.125) * 2.0 ** -30 * c
            for g in rng.permutation(8)[:4]:
                e = rng.choice([-1.0, 1.0], C) * 2.0 ** -30
                x[r, g, 8, :, 0] = 1.25 * e
                x[r, g, 9, :, 0] = -1.125 * e
        at = [0, C - 1, int(rng.integers(C)), int(rng.integers(C))]
        for g, j in zip(rng.permutation(8)[:4], at): x[r, g, 0, j, 0] = 2.0 ** 29 * rng.choice([-1.0, 1.0])
        k = 1.0 if o[r] == 0 else 2.0 ** -30
        for h in range(0, 128, 16):
            u[r, h, h, 0] = k
            if o[r] < 2: u[r, h + 11, h, 0] = k
            if o[r] < 3: u[r, h + 8, h] = k
            else:
                u[r, h + 8, h, 0] = k
                u[r, h + 9, h, 0] = 1.125 * k
                u[r, h + 12, h, 0] = k
    return {"x": x.reshape(N, 128, 4 * C).astype(BF), "u": u.reshape(N, 128, 512), "v": d["v"], **lists(rng), **weights(rng, w)}
def setup_inputs_odd(rng):
    d = numbers_of(rng)
    x = (1.0 + (2 * rng.integers(0, 64, (N, 16, 8, C, 4)) + 1) * 2.0 ** -7) * np.exp2(-rng.integers(0, 7, (N, 16, 8, C, 4)).astype(np.float64)) * rng.choice([-1.0, 1.0], (N, 16, 8, C, 4))
    x[:, :, 0, :, 0] = 1.96875 * 2.0 ** 8 * rng.choice([-1.0, 1.0], (N, 16, C))
    u = d["u"].reshape(N, 16, 8, 128, 4)
    u[:, :, 0, ::16] = 0
    for r in range(N):
        for n, g in enumerate(rng.permutation(8)[:4]):
            x[r, 2 * g, 1, :, 0] = (8 + rng.integers(0, 2, C)) * 2.0 ** (n % 2 - 8)
            u[r, :, :, 16 * g] = 0
            u[r, 2 * g, 1, 16 * g, 0] = 1.0
    return {"x": x.astype(np.float32).reshape(N, 128, 4 * C).astype(BF), "u": u.reshape(N, 128, 512), "v": d["v"], **lists(rng), **weights(rng, layers(rng, [0, 8]))}
def setup_inputs_ends(rng):
    d = numbers_of(rng)
    o, e = rng.permutation(N) % 4, rng.permutation(N) % 4
    x = np.zeros((N, 8, 16, C, 4))
    u = d["u"].astype(np.float32).reshape(N, 128, 128, 4)
    v = np.zeros((N, 128, 512))
    w = np.zeros((N, 128, 4, 128, 4), np.float32)
    still = int(rng.integers(8))
    i = np.arange(128)
    for r in range(N):
        h = rng.permutation(8)
        c = np.where(h < 2, 0.0, h % 2 * 2.0 - 1.0)[None, :, None]
        large = (0.88 + 0.04 * rng.random((8, 16, C, 4))) * 2.0 ** 30
        if o[r] == 0: x[r] = -large
        if o[r] == 1: x[r] = large * rng.choice([-1.0, 1.0], (C, 1))
        if o[r] == 2: x[r] = -(1.0 + 0.125 * rng.integers(0, 8, (8, 16, C, 4))) * 2.0 ** -30
        if o[r] == 3: x[r] = d["x"][r].astype(np.float32).reshape(8, 16, C, 4)[:, :, :1]
        if o[r] < 2: u[r, :, ::16] = c * (0.9 + 0.1 * rng.random((128, 8, 4))) * 2.0 ** 30
        if o[r] == 2: u[r, :, ::16] = c * (1.0 + 0.125 * rng.integers(0, 8, (128, 8, 4))) * 2.0 ** -30
        if o[r] == 3: u[r, :, ::16] *= np.abs(c).astype(np.float32)
        v[r] = rng.choice([-1.0, 1.0], (128, 512)) * (2.0 ** 30 if o[r] < 2 else 2.0 ** -30)
        k = np.array([0.125, 0.25, 0.5])[rng.permutation(8) % 3]
        if o[r] == 2: k[:] = 32.0
        if o[r] == 3: k[k == 0.125] = 2.0 ** -8
        k[still] = 256.0 if o[r] == 2 else 0.0
        for b in range(4): w[r, i, b, i, b] = k[i // 16]
    a, t, m = orders(rng), orders(rng), pairing(rng)
    j = np.arange(C)
    a[e == 0] = j
    t[e == 0] = j
    m[e == 0] = j ^ 1
    a[e == 1] = C - 1 - j
    t[e == 1] = C - 1 - j
    m[e == 1] = C - 1 - j
    a[e == 2] = (j + 1) % C
    t[e == 2] = (j + C - 1) % C
    m[e == 2] = (j + C // 2) % C
    return {"x": x.astype(np.float32).reshape(N, 128, 4 * C).astype(BF), "u": u.reshape(N, 128, 512).astype(BF), "v": v.astype(np.float32).astype(BF), **stored(a, t, m), **weights(rng, w.astype(BF))}
def setup_inputs_spread(rng):
    d = setup_inputs(rng)
    d["x"] = wide(rng, N, 128, 4 * C, cols=6)
    return d
def check_inputs(d):
    b = []
    for k in ("x", "u", "v"):
        a = np.abs(d[k].astype(np.float32))
        if not (np.isfinite(a).all() and ((a == 0) | (a >= 2.0 ** -30) & (a <= 2.0 ** 30)).all()): b.append("a value of " + k)
    none, least, most = [emit(mx_ref.quantize(np.full((128, 16), k, np.float32).astype(BF)))[1][0, 0] for k in (0.0, 2.0 ** -8, 2.0 ** 8)]
    for r in range(N):
        for k in ("la", "lb"):
            if (np.sort(entries(d[k][r])) != np.arange(C)).any(): b.append(k + ": not every number once")
        m = gentries(d["mt"][r])
        if not ((m >= 0) & (m < C)).all(): b.append("an entry of mt")
        elif (np.take_along_axis(m, m, axis=1) != np.arange(C)).any() or (m == np.arange(C)).any(): b.append("mt: not in pairs")
        if ((d["wc"][r] == 0x7F) | (d["wc"][r] == 0xFF)).any(): b.append("wc: a code that is no number")
        s = mx_ref.live(d["ws"][r])
        if ((s != none) & ((s < least) | (s > most))).any(): b.append("ws: a scale out of range")
        if (((d["wc"][r].reshape(16, 8, 512, 4) & 0x7F) != 0) & (s == none)[:, None, :, None]).any(): b.append("wc: a code other than zero under the scale of zeros")
    return b
def reference(x, u, v, la, lb, mt, wc, ws):
    qu = [mx_ref.quantize(u[r]) for r in range(N)]
    lay = [pk(wc[r], ws[r]) for r in range(N)]
    mate = [gentries(mt[r]) for r in range(N)]
    kept = [[entries(la[r]), entries(lb[r])] for r in range(N)]
    now = [x[r] for r in range(N)]
    here = np.tile(np.arange(C), (8, 1))
    ll = np.zeros((N, 8, C), np.float32)
    for step in STEP:
        went, sent = [], []
        for r in range(N):
            s = mx_ref.matmul(qu[r], mx_ref.quantize(now[r]))[::16] + np.float32(0.0)
            t = np.take_along_axis(s, mate[r], axis=1)
            crossed = np.where(here < mate[r], s < t, t < s)
            e = np.where(crossed, mate[r], here)
            a = [kept[r][0][e[0]], kept[r][1][e[7]]]
            kept[r] = a[:2]
            for g in range(1, 7):
                k = e[g][a[g]]
                a.append(a[g - 1][k[k]])
            went.append(np.stack(a))
            ll[r] = went[r]
            z = mx_ref.quantize(gcols(now[r], went[r]))
            sent.append(mx_ref.quantize(tile([mx_ref.matmul(pick(lay[r], np.arange(128 * b, 128 * b + 128)), z) * np.float32(0.03125) for b in range(4)])))
        made = []
        for r in range(N):
            far = gcols(decode(sent[r ^ step]).astype(BF), went[r][::-1])
            made.append((now[r].astype(np.float32) + far.astype(np.float32)).astype(BF))
        now = made
    y = np.zeros((N, 128, C), np.float32)
    oc, osc = np.zeros((N, 128, 4 * C), np.uint8), np.zeros((N, 16, C), np.uint8)
    for r in range(N):
        q = mx_ref.quantize(now[r])
        y[r] = mx_ref.matmul(mx_ref.quantize(v[r]), q)
        oc[r], osc[r] = emit(q)
    return {"y": y, "ll": ll, "oc": oc, "osc": osc}

from concourse.bass import DstId, RemoteDMATransfer, IndirectOffsetOnAxis
from concourse.mybir import dt, AluOpType, AxisListType, ActivationFunctionType

C, HALF, ROUNDS, STEP = 320, 160, 3, [4, 1, 2]
MID = 160
X4 = "float8_e4m3fn_x4"
SCRATCH = {
    "xi": ("sbuf", [128, 4 * C], "bfloat16"), "xp": ("sbuf", [128, 4 * C], "bfloat16"),
    "zt": ("sbuf", [128, 4 * C], "bfloat16"), "ht": ("sbuf", [128, 4 * C], "bfloat16"),
    "ut": ("sbuf", [128, 512], "bfloat16"), "vt": ("sbuf", [128, 512], "bfloat16"), "et": ("sbuf", [128, 4096], "bfloat16"),
    "uq": ("sbuf", [128, 128], X4), "us": ("sbuf", [128, 128], "uint8"), "u2q": ("sbuf", [128, 128], X4), "u2s": ("sbuf", [128, 128], "uint8"),
    "vq": ("sbuf", [128, 128], X4), "vs": ("sbuf", [128, 128], "uint8"),
    "wq": ("sbuf", [128, 512], X4), "wp": ("sbuf", [128, 512], "uint8"),
    "eq": ("sbuf", [128, 1024], X4), "es": ("sbuf", [128, 1024], "uint8"),
    "xq": ("sbuf", [128, C], X4), "xs": ("sbuf", [128, C], "uint8"),
    "zq": ("sbuf", [128, C], X4), "zs": ("sbuf", [128, C], "uint8"),
    "ssb": ("sbuf", [128, C], "float32"), "ssm": ("sbuf", [128, C], "float32"), "dd": ("sbuf", [128, C], "bfloat16"), "xt": ("sbuf", [128, C], "bfloat16"),
    "dm": ("sbuf", [128, 32], "float32"), "q0": ("sbuf", [128, 32], "float32"), "q1": ("sbuf", [128, 32], "float32"), "q2": ("sbuf", [128, 32], "float32"),
    "cb": ("sbuf", [128, 32], "float32"), "e32": ("sbuf", [128, 32], "bfloat16"), "xx": ("sbuf", [128, 64], "bfloat16"), "oo": ("sbuf", [128, 64], "bfloat16"),
    "eo": ("sbuf", [128, 64], "uint16"), "e7": ("sbuf", [128, 32], "uint16"), "do": ("sbuf", [128, 64], "uint16"),
    "idw": ("sbuf", [128, C], "bfloat16"), "mask": ("sbuf", [128, C], "bfloat16"), "keep": ("sbuf", [128, C], "bfloat16"),
    "ia": ("sbuf", [128, C], "int32"), "ib": ("sbuf", [128, C], "int32"), "ic": ("sbuf", [128, 512], "int32"), "pi": ("sbuf", [128, 32], "int32"), "pj": ("sbuf", [128, 32], "int32"), "pk": ("sbuf", [128, 32], "int32"), "ii": ("sbuf", [128, 32], "int32"),
    "pm": ("sbuf", [128, 8], "float32"), "pf": ("sbuf", [128, 32], "float32"),
    "mti": ("sbuf", [128, 32], "int32"), "mo": ("sbuf", [128, 32], "uint16"), "lab": ("sbuf", [128, 64], "int32"), "lao": ("sbuf", [128, 64], "uint16"), "uo": ("sbuf", [128, 16], "uint16"), "ui": ("sbuf", [128, 16], "int32"),
    "ee0": ("sbuf", [128, C], "bfloat16"), "ee1": ("sbuf", [128, C], "bfloat16"), "dd0": ("sbuf", [128, C], "bfloat16"), "dd1": ("sbuf", [128, C], "bfloat16"), "e6": ("sbuf", [128, C], "bfloat16"),
    "vv": ("sbuf", [128, C], "bfloat16"), "mm0": ("sbuf", [128, C], "bfloat16"), "mm1": ("sbuf", [128, C], "bfloat16"), "sc0": ("sbuf", [128, C], "bfloat16"), "sc1": ("sbuf", [128, C], "bfloat16"),
    "le": ("sbuf", [128, 32], "uint16"), "lo": ("sbuf", [128, 32], "uint16"), "pa": ("sbuf", [128, 32], "uint16"), "pb": ("sbuf", [128, 32], "uint16"), "ls": ("sbuf", [128, 32], "uint16"),
    "t0": ("sbuf", [128, 32], "float32"), "t1": ("sbuf", [128, 32], "float32"), "t2": ("sbuf", [128, 32], "float32"),
    "lle": ("sbuf", [128, C], "float32"), "llo": ("sbuf", [128, C], "float32"), "ysb": ("sbuf", [128, C], "float32"),
    "rlq": ("sbuf", [128, HALF], X4), "rls": ("sbuf", [128, HALF], "uint8"),
    "ps": ("psum", [128, 4096], "float32"),
}
for _k in range(1, 7):
    SCRATCH["w%d" % _k] = ("sbuf", [128, C], "bfloat16")
for _k in range(7):
    SCRATCH["k%d" % _k] = ("sbuf", [128, 32], "uint16")
for _r in range(ROUNDS):
    for _n in ("hq", "ld", "ga", "gb"):
        SCRATCH["%sc%d" % (_n, _r)] = ("sbuf", [128, C], X4)
        SCRATCH["%ss%d" % (_n, _r)] = ("sbuf", [128, C], "uint8")
QUEUES = ("V", "S", "P", "G")
SEMAPHORES = ["qV", "qS", "qP", "qG"] + ["dm%d" % k for k in range(16)] + ["arr%d" % r for r in range(ROUNDS)] + ["sent%d" % r for r in range(ROUNDS)] + ["hopq", "hops", "hopsent", "stored"]


def relays(core, dst, T, topo):
    return [c for c in topo.cores_of(core) if c != core and T.rank_of(c) is None and topo.die(c) == topo.die(core) and topo.may_write(c, dst)][:2]


def hand_on(g, core, T, topo):
    for r, s in enumerate(STEP):
        for i in range(len(T.cores)):
            src, dst = T.cores[i], T.cores[i ^ s]
            if topo.may_write(src, dst):
                continue
            rel = relays(src, dst, T, topo)
            if core not in rel:
                continue
            a = HALF * rel.index(core)
            n_in, m = len(topo.engines(src, core)), topo.mask(core, dst)
            rid, pid = topo.addr(dst, core)
            g.wait_ge(T.sem.hopq, n_in)
            g.remote_dma(T["ldc%d" % r][:, a:a + HALF].bitcast(dt.uint8), T.rlq[:, 0:HALF].bitcast(dt.uint8), T.sem["arr%d" % r], T.sem.hopsent, pid, rid, m)
            g.wait_ge(T.sem.hops, n_in)
            g.remote_dma(T["lds%d" % r][:, a:a + HALF], T.rls[:, 0:HALF], T.sem["arr%d" % r], T.sem.hopsent, pid, rid, m)
            g.wait_ge(T.sem.hopsent, 2 * len(topo.engines(core, dst)))


def rank_program(g, core, T, topo):
    rank = T.rank_of(core)
    if rank is None:
        return hand_on(g, core, T, topo)
    A, AF = AluOpType, ActivationFunctionType
    eng = {"V": g.vector, "S": g.scalar, "P": g.tensor, "G": g, "Y": g.sync}
    cnt, known, snap = {}, {q: {} for q in eng}, {}
    writers, readers = [], []

    def R(name, c0=0, c1=None, step=1, p0=0, p1=128, cast=None):
        c1 = (C if c1 is None else c1)
        ap = T[name][p0:p1, c0:c1] if step == 1 else T[name][p0:p1, c0:c1:step]
        if cast is not None:
            ap = ap.bitcast(cast)
        return ((name, p0, p1, c0, c1, step), ap)

    def hit(a, b):
        return (a[0] == b[0] and a[1] < b[2] and b[1] < a[2] and a[3] < b[4] and b[3] < a[4]
                and not (a[5] == b[5] and a[5] > 1 and (a[3] - b[3]) % a[5]))

    def inside(a, b):
        return a[0] == b[0] and b[1] <= a[1] and a[2] <= b[2] and b[3] <= a[3] and a[4] <= b[4] and (b[5] == 1 or (a[5] == b[5] and (a[3] - b[3]) % a[5] == 0))

    def waits(q, W, Rd, own_waw=True):
        need = {}
        for r in Rd:
            for (b, s, n) in writers:
                if hit(r[0], b):
                    need[s] = max(need.get(s, 0), n)
        for w in W:
            for (b, s, n) in writers + readers:
                if hit(w[0], b) and (own_waw or s != "q" + q):
                    need[s] = max(need.get(s, 0), n)
        k = known[q]
        need = {s: n for s, n in need.items() if k.get(s, 0) < n}
        for s in list(need):
            for s2 in list(need):
                if s2 != s and s in need and snap.get((s2, need[s2]), {}).get(s, 0) >= need[s]:
                    del need[s]
        for s, n in need.items():
            eng[q].wait_ge(T.sem[s], n)
            for a, b in snap.get((s, n), {}).items():
                k[a] = max(k.get(a, 0), b)
            k[s] = max(k.get(s, 0), n)

    def note(W, Rd, s, n):
        for w in W:
            writers[:] = [e for e in writers if not inside(e[0], w[0])]
            readers[:] = [e for e in readers if not inside(e[0], w[0])]
            writers.append((w[0], s, n))
        for r in Rd:
            readers[:] = [e for e in readers if not (e[1] == s and inside(e[0], r[0]))]
            readers.append((r[0], s, n))

    def op(q, call, W, Rd, own_waw=True):
        waits(q, W, Rd, own_waw)
        s = "q" + q
        cnt[s] = cnt.get(s, 0) + 1
        call().then_inc(T.sem[s], 1)
        snap[(s, cnt[s])] = dict(known[q])
        note(W, Rd, s, cnt[s])

    nd = [0]

    def dma(q, dst, src, ap=None, s=None):
        waits(q, [dst], [src] if src is not None else [])
        s = "dm%d" % nd[0]
        nd[0] += 1
        eng[q].dma_start(dst[1], src[1] if ap is None else ap).then_inc(T.sem[s], 16)
        snap[(s, 16)] = dict(known[q])
        note([dst], [], s, 16)

    stores = [0]

    def store(q, out, src):
        waits(q, [], [src])
        eng[q].dma_start(out, src[1]).then_inc(T.sem.stored, 16)
        stores[0] += 16

    def tt(o, a, b, f, q="V", off=None):
        op(q, lambda: eng[q].tensor_tensor(o[1], a[1] if off is None else a[1].indirect(off[1]), b[1], f), [o], [a, b] + ([off] if off else []))

    def ts(o, a, s1, f, s2=None, f2=None, extra=[]):
        if f2 is None:
            op("V", lambda: g.vector.tensor_scalar(o[1], a[1], s1, None, f), [o], [a] + extra)
        else:
            op("V", lambda: g.vector.tensor_scalar(o[1], a[1], s1, s2, f, f2), [o], [a] + extra)

    def cp(q, o, a, off=None, scale=None, bias=None):
        src = a[1] if off is None else a[1].indirect(off[1])
        rd = [a] + ([off] if off else [])
        if q == "V":
            op("V", lambda: g.vector.tensor_copy(o[1], src), [o], rd)
        elif bias is not None:
            op("S", lambda: g.scalar.activation(o[1], src, AF.Identity, bias=bias), [o], rd)
        elif scale is not None:
            op("S", lambda: g.scalar.activation(o[1], src, AF.Copy, scale=scale), [o], rd)
        else:
            op("S", lambda: g.scalar.activation(o[1], src, AF.Copy), [o], rd)

    def tr(o, a):
        op("V", lambda: g.vector.transpose(o[1], a[1]), [o], [a])

    def fill(o, v):
        op("V", lambda: g.vector.memset(o[1], v), [o], [])

    def iota(o, pat, base, cm, flag=False):
        if flag:
            op("G", lambda: g.iota(o[1], pat, base, cm, allow_small_or_imprecise_dtypes=True), [o], [])
        else:
            op("G", lambda: g.iota(o[1], pat, base, cm), [o], [])

    def quant(qc, qs, a, b, tile, ta=None):
        ta = 4 * a if ta is None else ta
        o, s, i = R(qc, a, b), R(qs, a, b), R(tile, ta, ta + 4 * (b - a))
        op("V", lambda: g.vector.quantize_mx(o[1], s[1], i[1]), [o, s], [i])

    def mm(bank, n, lq, lsc, la, rq, rsc, ra, start=True, stop=True):
        o = R("ps", 512 * bank, 512 * bank + n)
        a, b, c, d = R(lq, la, la + 128), R(lsc, la, la + 128), R(rq, ra, ra + n), R(rsc, ra, ra + n)
        op("P", lambda: g.tensor.matmul_mx(o[1], a[1], b[1], c[1], d[1], start, stop), [o], [a, b, c, d], own_waw=start)

    def bank(k, n=HALF):
        return R("ps", 512 * k, 512 * k + n)

    def offs(name, a=0):
        return R(name, a, a + 20)

    def fold(win, off, k):
        tt(R("mm%d" % k), R(win), R("mask"), A.mult, off=off)

    def scan(k):
        o, d0, d1 = R("sc%d" % k), R("keep"), R("mm%d" % k)
        op("V", lambda: g.vector.tensor_tensor_scan(o[1], d0[1], d1[1], 0.0, A.mult, A.add), [o], [d0, d1])

    def conv(dst, blk, k, src):
        ts(R(dst, 0, 20, 1, 32 * blk, 32 * blk + 32), R("sc%d" % k, 15, C, 16, 32 * src, 32 * src + 32), float(MID), A.add)

    L = lambda name: ((name + "!", 0, 1, 0, 1, 1), T[name])
    fill(R("lab", 0, 64), 0)
    for n in ("k0", "k1", "k2", "k3", "k4", "k5", "k6", "le", "lo", "e7", "pa", "pb"):
        fill(R(n, 0, 32), 0)
    fill(R("e32", 0, 32), 0.0)
    fill(R("e6"), 0.0)
    dma("Y", R("xi", 0, 640), None, T.x[:, 0:640])
    dma("S", R("xi", 640, 1280), None, T.x[:, 640:1280])
    dma("Y", R("ut", 0, 512), None, T.u[:, :])
    dma("S", R("mti", 0, 20), None, T.mt[:, :])
    for h in range(2):
        dma("Y", R("lab", 0, 20, 1, 16 * h, 16 * h + 16), None, T.la[:, :])
        dma("S", R("lab", 20, 40, 1, 16 * h, 16 * h + 16), None, T.lb[:, :])
    dma("Y", R("wq", 0, 512, cast=dt.uint8), None, T.wc[:, :])
    dma("Y", R("wp", 0, 512), None, T.ws[:, :])
    dma("Y", R("vt", 0, 512), None, T.v[:, :])
    iota(R("idw"), [[1, C]], -MID, 0, True)
    iota(R("ui", 0, 8), [[16, 8]], 0, 0)
    iota(R("pi", 0, 20), [[0, 20]], 0, 1)
    iota(R("pj", 0, 20), [[32, 10], [0, 2]], -MID, 0)
    iota(R("pk", 0, 20), [[16, 20]], 0, 0)
    iota(R("ia"), [[-1, C]], 336, 1)
    iota(R("ib"), [[1, C]], 0, 0)
    iota(R("ic", 0, 512), [[1, 512]], 0, -4)
    cp("V", R("uo", 0, 8), R("ui", 0, 8))
    ts(R("ii", 0, 20), R("pi", 0, 20), 31, A.bitwise_and)
    tt(R("cb", 0, 20), R("ii", 0, 20), R("pj", 0, 20), A.add)
    ts(R("ii", 0, 20), R("pi", 0, 20), 15, A.bitwise_and)
    tt(R("pf", 0, 20), R("ii", 0, 20), R("pk", 0, 20), A.add)
    cp("V", R("do", 0, 20), R("pf", 0, 20))
    cp("V", R("do", 20, 40), R("pf", 0, 20))
    ts(R("ii", 0, 4), R("pi", 0, 4), 16, A.bitwise_and)
    ts(R("pm", 0, 4), R("ii", 0, 4), 0.0, A.is_equal)
    ts(R("pm", 4, 8), R("ii", 0, 4), 0.0, A.is_gt)
    quant("uq", "us", 0, 128, "ut")
    op("V", lambda: g.vector.tensor_copy(T.u2q[:, 0:128].bitcast(dt.uint32), T.uq[:, 0:128].bitcast(dt.uint32).indirect(T.uo[:, 0:8])), [R("u2q", 0, 128)], [R("uq", 0, 128), R("uo", 0, 8)])
    op("V", lambda: g.vector.tensor_copy(T.u2s[:, 0:128], T.us[:, 0:128].indirect(T.uo[:, 0:8])), [R("u2s", 0, 128)], [R("us", 0, 128), R("uo", 0, 8)])
    m0, m1 = R("pm", 0, 1), R("pm", 4, 5)

    def scores():
        for h in range(2):
            quant("xq", "xs", HALF * h, HALF * h + HALF, "xi")
            mm(4 * h, HALF, "u2q", "u2s", 0, "xq", "xs", HALF * h)

    scores()
    cp("V", R("mo", 0, 20), R("mti", 0, 20))
    cp("V", R("lao", 0, 40), R("lab", 0, 40))
    cp("S", R("w1"), R("idw"), offs("lao"))
    cp("S", R("w2"), R("idw"), offs("lao", 20))
    cp("V", R("vv"), R("idw"), offs("mo"))
    tr(R("xt"), R("vv"))
    tt(R("dm", 0, 20), R("xt", 0, C, 16), R("cb", 0, 20), A.subtract)
    ts(R("ia"), R("ia"), 15, A.bitwise_and)
    ts(R("mask"), R("ia"), 0.0, A.is_equal)
    ts(R("ib"), R("ib"), 15, A.bitwise_and)
    ts(R("keep"), R("ib"), 0.0, A.is_gt)

    def send(r, h):
        dst = T.cores[rank ^ STEP[r]]
        a = HALF * h
        ld = ("ldc%d" % r, "lds%d" % r, T.sem["arr%d" % r], T.sem["arr%d" % r], a)
        to = dst
        if not topo.may_write(core, dst):
            to = relays(core, dst, T, topo)[h]
            ld = ("rlq", "rls", T.sem.hopq, T.sem.hops, 0)
        rid, pid = topo.addr(to, core)
        m = topo.mask(core, to)
        hc, hs = R("hqc%d" % r, a, a + HALF, cast=dt.uint8), R("hqs%d" % r, a, a + HALF)
        waits("G", [], [hc, hs])
        g.remote_dma(T[ld[0]][:, ld[4]:ld[4] + HALF].bitcast(dt.uint8), hc[1], ld[2], T.sem["sent%d" % r], pid, rid, m)
        g.remote_dma(T[ld[1]][:, ld[4]:ld[4] + HALF], hs[1], ld[3], T.sem["sent%d" % r], pid, rid, m)
        return 2 * len(topo.engines(core, to))

    def arrivals(r):
        src = T.cores[rank ^ STEP[r]]
        n = 0
        for h in range(2):
            via = src if topo.may_write(src, core) else relays(src, core, T, topo)[h]
            n += 2 * len(topo.engines(via, core))
        return n

    sent = []
    for r in range(ROUNDS):
        last = r == ROUNDS - 1
        cp("S", R("ssb", 0, HALF), bank(0))
        cp("V", R("ssb", HALF, C), bank(4))
        cp("V", R("ssm", 0, HALF), R("ssb"), R("mo", 0, 10))
        cp("S", R("ssm", HALF, C), R("ssb"), R("mo", 10, 20))
        tt(R("dd", 0, HALF), R("ssm", 0, HALF), bank(0), A.subtract)
        tt(R("dd", HALF, C), R("ssm", HALF, C), bank(4), A.subtract)
        for t in range(4):
            cp("S", R("xp", C * t, C * t + C), R("xi", t, 4 * C, 4))
        tr(R("xt"), R("dd"))
        tt(R("q0", 0, 20), R("xt", 0, C, 16), R("dm", 0, 20), A.mult)
        ts(R("q1", 0, 20), R("q0", 0, 20), 0.0, A.is_gt)
        tt(R("q2", 0, 20), R("q1", 0, 20), R("dm", 0, 20), A.mult)
        tt(R("e32", 0, 10), R("q2", 0, 20, 2), R("cb", 0, 20, 2), A.add)
        tt(R("e32", 10, 20), R("q2", 1, 20, 2), R("cb", 0, 20, 2), A.add)
        tr(R("xx", 16, 48), R("e32", 0, 32))
        cp("V", R("xx", 0, 16), R("xx", 16, 32))
        cp("V", R("xx", 48, 64), R("xx", 32, 48))
        tr(R("oo", 0, 64), R("xx", 0, 64))
        ts(R("eo", 0, 40, 2), R("oo", 0, 20), float(MID), A.add)
        ts(R("eo", 1, 40, 2), R("oo", 32, 52), float(MID), A.add)
        cp("S", R("ee0"), R("idw"), offs("eo"))
        cp("S", R("ee1"), R("idw"), offs("eo", 20))
        iota(R("ee0", 0, C, 1, 0, 32), [[1, C]], -MID, 0, True)
        fold("w1", offs("eo"), 0)
        cp("V", R("e7", 0, 20, 1, 0, 32), R("eo", 20, 40, 1, 96, 128))
        scan(0)
        fold("w2", offs("e7"), 1)
        conv("k0", 0, 0, 0)
        conv("k0", 1, 0, 0)
        scan(1)
        conv("le", 0, 0, 0)
        conv("lo", 0, 1, 0)
        for b in range(3):
            cp("V", R("do", 0, 40, 1, 32 * b + 32, 32 * b + 64), R("eo", 0, 40, 1, 32 * b, 32 * b + 32))
        cp("S", R("w1"), R("ee0"), offs("k0"))
        fold("ee1", offs("lo"), 0)
        cp("S", R("dd1"), R("ee1"), offs("do", 20))
        scan(0)
        conv("k1", 0, 0, 0)
        conv("k1", 1, 0, 0)
        cp("S", R("dd0"), R("ee0"), offs("do"))
        nextwin = {1: "dd1", 2: "ee0", 3: "ee1", 4: "dd0", 5: "e6"}
        kblock = {1: 1, 2: 1, 3: 0, 4: 0, 5: 0}
        split = {1: 0, 2: 96, 3: 160, 4: 160, 5: 160, 6: 192}
        for s in range(1, 7):
            k, w = "k%d" % s, "w%d" % s
            n = C - split[s]
            cp("V", R("vv", 0, n), R(w), R(k, 0, n // 16))
            if split[s]:
                cp("S", R("vv", n, C), R(w), R(k, n // 16, 20))
            if s < 6:
                cp("S", R("w%d" % (s + 1)), R(nextwin[s]), offs(k))
            if s == 1:
                cp("S", R("ee0", 0, C, 1, 0, 32), R("dd0", 0, C, 1, 64, 96))
            if s == 2:
                cp("S", R("ee1", 0, C, 1, 0, 32), R("dd1", 0, C, 1, 64, 96))
            if s == 3:
                cp("S", R("dd0", 0, C, 1, 0, 32), R("dd0", 0, C, 1, 96, 128))
                cp("S", R("dd0", 0, C, 1, 32, 64), R("ee0", 0, C, 1, 64, 96))
            if s == 4:
                cp("S", R("e6", 0, C, 1, 0, 32), R("ee1", 0, C, 1, 64, 96))
            fold("vv", offs(k), s % 2)
            scan(s % 2)
            if s < 6:
                kb = kblock[s]
                conv("k%d" % (s + 1), 0, s % 2, kb)
                conv("k%d" % (s + 1), 1, s % 2, kb)
                li = s + 1
                conv("le" if li % 2 == 0 else "lo", li // 2, s % 2, 1 - kb)
                if s == 5:
                    ts(R("t0", 0, 20), R("le", 0, 20), m0[1], A.mult, extra=[m0])
                    ts(R("t1", 0, 20, 1, 0, 64), R("lo", 0, 20, 1, 0, 64), T.pm[0:64, 4:5], A.mult, extra=[m1])
                    ts(R("t1", 0, 20, 1, 64, 96), R("lo", 0, 20, 1, 64, 96), T.pm[64:96, 4:5], A.mult, extra=[m1])
            else:
                ts(R("t1", 0, 20, 1, 96, 128), R("sc0", 15, C, 16, 0, 32), float(MID), A.add, T.pm[0:32, 4:5], A.mult, extra=[m1])
                tt(R("t2", 0, 20), R("t0", 0, 20), R("t1", 0, 20), A.add)
                cp("V", R("ls", 0, 20), R("t2", 0, 20))
        for h in range(2):
            for t in range(4):
                cp("V" if t < 2 else "S", R("zt", 640 * h + t, 640 * h + 640, 4), R("xp", C * t, C * t + C), R("ls", 10 * h, 10 * h + 10))
            quant("zq", "zs", HALF * h, HALF * h + HALF, "zt")
            for b in range(4):
                mm(4 * h + b, HALF, "wq", "wp", 128 * b, "zq", "zs", HALF * h)
        for b in range(4):
            cp("S", R("ht", b, 640, 4), bank(b), scale=0.03125)
        n_sent = 0
        for h in range(2):
            if h == 1:
                for b in range(4):
                    ts(R("ht", 640 + b, 1280, 4), bank(4 + b), 0.03125, A.mult)
            quant("hqc%d" % r, "hqs%d" % r, HALF * h, HALF * h + HALF, "ht")
            n_sent += send(r, h)
        sent.append(n_sent)
        conv("lo", 3, 0, 0)
        for b in range(4):
            cp("V", R("pa", 0, 20, 1, 32 * b, 32 * b + 32), R("lo", 0, 20, 1, 96 - 32 * b, 128 - 32 * b))
            cp("V", R("pb", 0, 20, 1, 32 * b, 32 * b + 32), R("le", 0, 20, 1, 96 - 32 * b, 128 - 32 * b))
        if r == 0:
            for par in range(2):
                for b in range(4):
                    k = 4 * par + b
                    ts(R("et", 512 * k, 512 * k + 512), R("ic", 0, 512), float(b), A.is_equal, (m0, m1)[par][1], A.mult, extra=[(m0, m1)[par]])
                    quant("eq", "es", 128 * k, 128 * k + 128, "et")
            quant("vq", "vs", 0, 128, "vt")
        if last:
            cp("S", R("lle"), R("idw"), offs("le"), bias=float(MID))
            cp("S", R("llo"), R("idw"), offs("lo"), bias=float(MID))
            for b in range(4):
                store("Y", T.ll[2 * b:2 * b + 1, :], R("lle", 0, C, 1, 32 * b, 32 * b + 1))
                store("Y", T.ll[2 * b + 1:2 * b + 2, :], R("llo", 0, C, 1, 32 * b, 32 * b + 1))
        ldc, lds = R("ldc%d" % r, cast=dt.uint32), R("lds%d" % r)
        note([ldc, lds], [], "arr%d" % r, arrivals(r))
        for h in range(2):
            for n, ls in (("ga", "pa"), ("gb", "pb")):
                off = R(ls, 10 * h, 10 * h + 10)
                cp("V", R("%sc%d" % (n, r), HALF * h, HALF * h + HALF, cast=dt.uint32), ldc, off)
                cp("S", R("%ss%d" % (n, r), HALF * h, HALF * h + HALF), lds, off)
        for h in range(2):
            for b in range(4):
                mm(4 * h + b, HALF, "eq", "es", 128 * b, "gac%d" % r, "gas%d" % r, HALF * h, True, False)
                mm(4 * h + b, HALF, "eq", "es", 512 + 128 * b, "gbc%d" % r, "gbs%d" % r, HALF * h, False, True)
        for h in range(2):
            for b in range(4):
                x = R("xi", 640 * h + b, 640 * h + 640, 4)
                tt(x, bank(4 * h + b), x, A.add)
            quant("xq", "xs", HALF * h, HALF * h + HALF, "xi")
            if last:
                mm(4 * h, HALF, "vq", "vs", 0, "xq", "xs", HALF * h)
            else:
                mm(4 * h, HALF, "u2q", "u2s", 0, "xq", "xs", HALF * h)
    for h in range(2):
        a = HALF * h
        cp("S" if h == 0 else "V", R("ysb", a, a + HALF), bank(4 * h))
        store("Y", T.oc[:, 4 * a:4 * a + 4 * HALF], R("xq", a, a + HALF, cast=dt.uint8))
        for k in range(4):
            store("S" if k % 2 else "Y", T.osc[4 * k:4 * k + 4, a:a + HALF], R("xs", a, a + HALF, 1, 32 * k, 32 * k + 4))
        store("Y", T.y[:, a:a + HALF], R("ysb", a, a + HALF))
    for r in range(ROUNDS):
        g.wait_ge(T.sem["sent%d" % r], sent[r])
    for q in QUEUES:
        if cnt.get("q" + q, 0):
            g.wait_ge(T.sem["q" + q], cnt["q" + q])
    for k in range(nd[0]):
        g.wait_ge(T.sem["dm%d" % k], 16)
    g.wait_ge(T.sem.stored, stores[0])
